import numpy as np, ml_dtypes
CORES = [78,86,94,102,110,118]
N = 6
import mx_ref
BF = ml_dtypes.bfloat16
def entries(a):
    return np.ascontiguousarray(a.T).reshape(-1)
def table(e):
    return np.ascontiguousarray(np.reshape(e, (-1, 16)).T).astype(np.int32)
def cut(t, i, w=512):
    return t[:, w * i:w * i + w]
def f(rng, *shape):
    return mx_ref.flush((rng.standard_normal(shape, dtype=np.float32) * np.exp2(rng.integers(-2, 3, shape[:-1] + (1,)))).astype(BF))
def wide(rng, *shape, cols=0):
    v = rng.standard_normal(shape, dtype=np.float32) * np.exp2(rng.integers(-12, 13, shape)).astype(np.float32)
    if cols: v *= np.repeat(np.exp2(rng.integers(-cols, cols + 1, shape[:-2] + (1, shape[-1] // 4))) * (rng.random(shape[:-2] + (1, shape[-1] // 4)) > 0.0625), 4, axis=-1).astype(np.float32)
    return mx_ref.flush(v.astype(BF))
SH, CH, R = 192, 32, 3
def lists(rng, how=""):
    o = []
    for q in range(N):
        p = rng.permutation(SH); h = int(rng.integers(0, 2)); e = []
        for t in range(R):
            if how == "same": v = p[:CH]
            elif how == "apart": v = p[CH * t:CH * t + CH]
            elif how == "ends": v = np.arange(CH) + (SH - CH) * ((h + t) % 2)
            elif how == "pairs": v = p[CH:2 * CH] if t >= 2 - h else p[:CH]
            else: v = rng.permutation(SH)[:CH]
            e.append(rng.permutation(v))
        o.append(table(np.concatenate(e)))
    return np.stack(o)
def fit(v):
    v = np.array(v); v[np.abs(v.astype(np.float32)) < np.float32(2.0 ** -30)] = 0
    return v
def setup_inputs(rng):
    return {"x": f(rng, N, 128, 512 * (R + 1)), "wm": f(rng, N, 128, 4 * SH), "dl": f(rng, N, 128, 4 * R * CH), "ix": lists(rng)}
def setup_inputs_same(rng):
    d = setup_inputs(rng); d["ix"] = lists(rng, "same"); return d
def setup_inputs_apart(rng):
    d = setup_inputs(rng); d["ix"] = lists(rng, "apart"); return d
def setup_inputs_ends(rng):
    d = setup_inputs(rng); d["ix"] = lists(rng, "ends"); return d
def setup_inputs_pairs(rng):
    d = setup_inputs(rng); d["ix"] = lists(rng, "pairs"); return d
def setup_inputs_spread(rng):
    d = setup_inputs(rng); d["wm"] = fit(wide(rng, N, 128, 4 * SH, cols=6)); d["dl"] = fit(wide(rng, N, 128, 4 * R * CH, cols=6)); return d
def check_inputs(d):
    b = []
    for n in ("x", "wm", "dl"):
        v = np.abs(np.asarray(d[n]).astype(np.float32))
        if not np.isfinite(v).all() or ((v > 0) & ((v < 2.0 ** -30) | (v > 2.0 ** 30))).any(): b.append(n)
    for q in range(N):
        e = entries(d["ix"][q])
        if e.min() < 0 or e.max() >= SH or any(len(set(e[CH * t:CH * t + CH].tolist())) != CH for t in range(R)): b.append("ix")
    return b
def reference(x, wm, dl, ix):
    X = [[mx_ref.quantize(np.ascontiguousarray(cut(x[r], t))) for t in range(R + 1)] for r in range(N)]
    y = np.zeros((N, 128, (R + 1) * N * SH), np.float32)
    for q in range(N):
        W = np.array(wm[q]).reshape(128, SH, 4); new = np.array(dl[q]).reshape(128, R * CH, 4); e = entries(ix[q])
        for t in range(R + 1):
            if t: W[:, e[CH * (t - 1):CH * t]] = new[:, CH * (t - 1):CH * t]
            held = mx_ref.quantize(np.array(W).reshape(128, 4 * SH)); k = SH * (t * N + q)
            for r in range(N): y[r][:, k:k + SH] = mx_ref.matmul(X[r][t], held)
    return {"y": y}

@@ -1,0 +1,337 @@
+from concourse.bass import DstId, RemoteDMATransfer
+from concourse.mybir import dt, AluOpType, ActivationFunctionType
+
+N, SH, CH, R = 6, 192, 32, 3
+ND = R * CH
+NP = ND + SH
+TC = SH // 16
+LC = R * TC
+SLOTS = range(1, N)
+
+SCRATCH = {
+    "wt": ("sbuf", [128, 4 * NP], "bfloat16"),
+    "xs": ("sbuf", [128, 512 * (R + 1)], "bfloat16"),
+    "xq": ("sbuf", [128, 128 * (R + 1)], "float8_e4m3fn_x4"),
+    "xqs": ("sbuf", [128, 128 * (R + 1)], "uint8"),
+    "pool": ("sbuf", [128, NP], "float8_e4m3fn_x4"),
+    "pools": ("sbuf", [128, NP], "uint8"),
+    "hop": ("sbuf", [128, NP], "float8_e4m3fn_x4"),
+    "hops": ("sbuf", [128, NP], "uint8"),
+    "ixa": ("sbuf", [128, ND], "int32"),
+    "ixr": ("sbuf", [128, ND], "int32"),
+    "ixb": ("sbuf", [128, ND], "bfloat16"),
+    "stepc": ("sbuf", [128, ND], "bfloat16"),
+    "pnum": ("sbuf", [128, TC], "int32"),
+    "plow": ("sbuf", [128, TC], "int32"),
+    "mnum": ("sbuf", [128, TC], "int32"),
+    "ccol": ("sbuf", [128, TC], "float32"),
+    "first": ("sbuf", [128, TC], "float32"),
+    "ne": ("sbuf", [128, TC * ND], "bfloat16"),
+    "stt": ("sbuf", [128, TC * ND], "bfloat16"),
+    "tab": ("sbuf", [128, LC], "uint16"),
+    "tabd": ("dram", [128, LC // 4], "uint16"),
+    "ys": ("sbuf", [128, (R + 1) * N * SH], "float32"),
+    "acc": ("psum", [128, 8 * 512], "float32"),
+}
+for _s in range(N):
+    SCRATCH["pk%d" % _s] = ("sbuf", [128, R * SH], "float8_e4m3fn_x4")
+    SCRATCH["pks%d" % _s] = ("sbuf", [128, R * SH], "uint8")
+for _s in SLOTS:
+    SCRATCH["land%d" % _s] = ("sbuf", [128, NP], "float8_e4m3fn_x4")
+    SCRATCH["lands%d" % _s] = ("sbuf", [128, NP], "uint8")
+    SCRATCH["off%d" % _s] = ("sbuf", [128, LC], "uint16")
+    if _s > 1:
+        SCRATCH["lst%d" % _s] = ("dram", [128, LC // 4], "uint16")
+
+SEMAPHORES = (["ldw", "ldi", "pb", "num", "vc", "qd", "tab", "tabd", "xl0", "xl1", "xq0", "xq1", "sent", "st", "hc", "hs"]
+              + ["ar%d" % s for s in SLOTS] + ["ls%d" % s for s in SLOTS] + ["rp%d" % s for s in SLOTS if s > 1]
+              + ["%s%d%d" % (k, s, t) for k in ("pv", "ps") for s in range(N) for t in (1, 2, 3)]
+              + ["%s%d%d" % (k, s, t) for k in ("mm", "ev") for s in range(N) for t in range(R + 1)])
+
+
+def source(r, s):
+    a, e = r // 2, r % 2
+    return 2 * ((a + s // 2) % (N // 2)) + (e if s % 2 == 0 else 1 - e)
+
+
+def dest(q, s):
+    return [r for r in range(N) if source(r, s) == q][0]
+
+
+def bits(engines):
+    m = 0
+    for e in engines:
+        m |= 1 << e
+    return m
+
+
+def relays(core, cores, topo):
+    q = cores.index(core)
+    mine = [c for c in topo.cores_of(core) if c != core]
+    a = [c for c in mine if topo.die(c) != topo.die(core)
+         and all(topo.may_write(c, cores[dest(q, s)]) for s in (3, 5))][0]
+    b = [c for c in mine if topo.die(c) == topo.die(core) and topo.may_write(c, cores[dest(q, 4)])][0]
+    return a, b
+
+
+def rank_program(g, core, T, topo):
+    cores = list(T.cores)
+    rank = T.rank_of(core)
+
+    def at(c):
+        a = topo.addr(c)
+        return DstId(rid=a[0], pnc=a[1])
+
+    def send(src, dst, sem, to, engines):
+        a = topo.addr(to)
+        g.remote_dma(dst, src, sem, T.sem.sent, a[1], a[0], bits(engines))
+        return len(engines)
+
+    if rank is None:
+        for q, c in enumerate(cores):
+            if core not in topo.cores_of(c):
+                continue
+            a, b = relays(c, cores, topo)
+            slots = (3, 5) if core == a else (4,) if core == b else ()
+            n = 0
+            for s in slots:
+                to = cores[dest(q, s)]
+                eng = topo.engines(core, to)
+                if s == slots[0]:
+                    g.wait_ge(T.sem.hc, len(relay_engines(c, core, cores, topo)))
+                n += send(T.hop[:].bitcast(dt.uint8), T["land%d" % s][:].bitcast(dt.uint8), T.sem["ar%d" % s], to, eng)
+                if s == slots[0]:
+                    g.wait_ge(T.sem.hs, len(relay_engines(c, core, cores, topo)))
+                n += send(T.hops[:], T["lands%d" % s][:], T.sem["ar%d" % s], to, eng)
+            if n:
+                g.wait_ge(T.sem.sent, n)
+        return
+
+    V, S, P, Y = g.vector, g.scalar, g.tensor, g.sync
+    relay_a, relay_b = relays(core, cores, topo)
+    far = [None] + [cores[dest(rank, s)] for s in SLOTS]
+    off_eng = topo.engines(core, far[1])
+
+    Y.dma_start(T.wt[:, 4 * ND:4 * NP], T.wm[:]).then_inc(T.sem.ldw, 16)
+    S.dma_start(T.wt[:, 0:4 * ND], T.dl[:]).then_inc(T.sem.ldw, 16)
+    for t in range(R):
+        S.dma_start(T.ixa[0:1, CH * t:CH * t + CH], T.ix[:, 2 * t:2 * t + 2]).then_inc(T.sem.ldi, 16)
+    h = 256 * (R + 1)
+    for i in range(2):
+        Y.dma_start(T.xs[:, h * i:h * i + h], T.x[:, h * i:h * i + h]).then_inc(T.sem["xl%d" % i], 16)
+
+    g.iota(T.pnum[:], [[0, TC]], 0, 1).then_inc(T.sem.num, 1)
+    g.iota(T.mnum[:], [[16, TC]], 0, 0).then_inc(T.sem.num, 1)
+    g.wait_ge(T.sem.ldi, 16 * R)
+    g.partition_broadcast(T.ixr[:], T.ixa[0:1, :], 128).then_inc(T.sem.pb, 1)
+
+    sent = 0
+
+    def two(s, relay):
+        n = 0
+        out, on = topo.engines(core, far[s]), relay_engines(core, relay, cores, topo)
+        for src, land, sem_l, hop, sem_h in (
+                (T.pool[:].bitcast(dt.uint8), T["land%d" % s][:].bitcast(dt.uint8), T.sem["ar%d" % s],
+                 T.hop[:].bitcast(dt.uint8), T.sem.hc),
+                (T.pools[:], T["lands%d" % s][:], T.sem["ar%d" % s], T.hops[:], T.sem.hs)):
+            g.remote_dma_fused([
+                RemoteDMATransfer(dst_ids=[at(far[s])], dma_engine_mask=bits(out), remote_sem=sem_l, srcs=[src], dsts=[land]),
+                RemoteDMATransfer(dst_ids=[at(relay)], dma_engine_mask=bits(on), remote_sem=sem_h, srcs=[src], dsts=[hop]),
+            ], local_sem=T.sem.sent)
+            n += len(out) + len(on)
+        return n
+
+    g.wait_ge(T.sem.qd, 1)
+    sent += two(1, relay_a)
+    g.wait_ge(T.sem.tab, R)
+    sent += send(T.tab[:], T.off1[:], T.sem.ls1, far[1], off_eng)
+    sent += two(2, relay_b)
+    g.wait_ge(T.sem.tabd, 16)
+    share = len(off_eng) // (N - 2)
+    tr = []
+    for i, s in enumerate(range(2, N)):
+        e = topo.engines(core, far[s])[share * i:share * i + share]
+        tr.append(RemoteDMATransfer(dst_ids=[at(far[s])], dma_engine_mask=bits(e), remote_sem=T.sem["ls%d" % s],
+                                    srcs=[T.tabd[:]], dsts=[T["lst%d" % s][:]]))
+        sent += len(e)
+    g.remote_dma_fused(tr, local_sem=T.sem.sent)
+    g.wait_ge(T.sem.sent, sent)
+
+    vc = [0]
+
+    def v(ins):
+        vc[0] += 1
+        ins.then_inc(T.sem.vc, 1)
+
+    def vwait():
+        V.wait_ge(T.sem.vc, vc[0])
+
+    v(V.memset(T.stepc[:, 0:ND:2], 16.0))
+    for t in range(R):
+        v(V.memset(T.stepc[:, CH * t + 1:CH * t + CH - 1:2], -15.0))
+    v(V.memset(T.stepc[:, CH - 1:ND:CH], 1.0))
+    V.wait_ge(T.sem.num, 2)
+    v(V.tensor_scalar(T.plow[:], T.pnum[:], 15, None, AluOpType.bitwise_and))
+    vwait()
+    v(V.tensor_tensor(T.ccol[:], T.plow[:], T.mnum[:], AluOpType.add))
+    vwait()
+    v(V.tensor_scalar(T.first[:], T.ccol[:], -1.0, float(-ND), AluOpType.mult, AluOpType.add))
+
+    V.wait_ge(T.sem.ldw, 32)
+    V.quantize_mx(T.pool[:], T.pools[:], T.wt[:]).then_inc(T.sem.qd, 1)
+
+    V.wait_ge(T.sem.pb, 1)
+    v(V.tensor_copy(T.ixb[:], T.ixr[:]))
+    vwait()
+    for m in range(TC):
+        v(V.tensor_scalar(T.ne[:, ND * m:ND * m + ND], T.ixb[:], T.ccol[:, m:m + 1], None, AluOpType.not_equal))
+    vwait()
+    for m in range(TC):
+        k = slice(ND * m, ND * m + ND)
+        v(V.tensor_tensor_scan(T.stt[:, k], T.ne[:, k], T.stepc[:], T.first[:, m:m + 1], AluOpType.mult, AluOpType.add))
+    vwait()
+    for t in range(1, R + 1):
+        V.tensor_scalar(T.tab[:, TC * (t - 1):TC * t], T.stt[:, CH * t - 1:TC * ND:ND], -1.0, float(CH * t),
+                        AluOpType.mult, AluOpType.add).then_inc(T.sem.tab, 1)
+
+    for i in range(2):
+        V.wait_ge(T.sem["xl%d" % i], 16)
+        k = slice(128 * (R + 1) // 2 * i, 128 * (R + 1) // 2 * (i + 1))
+        V.quantize_mx(T.xq[:, k], T.xqs[:, k], T.xs[:, h * i:h * i + h]).then_inc(T.sem["xq%d" % i], 1)
+
+    codes = [T.pool] + [T["land%d" % s] for s in SLOTS]
+    scales = [T.pools] + [T["lands%d" % s] for s in SLOTS]
+    offs = [T.tab] + [T["off%d" % s] for s in SLOTS]
+    eng = len(off_eng)
+
+    def have(q, s):
+        if s == 0:
+            q.wait_ge(T.sem.qd, 1)
+        else:
+            q.wait_ge(T.sem["ar%d" % s], 2 * eng)
+
+    def listed(q, s):
+        if s == 0:
+            q.wait_ge(T.sem.tab, R)
+        elif s == 1:
+            q.wait_ge(T.sem.ls1, eng)
+        else:
+            q.wait_ge(T.sem["rp%d" % s], 64)
+
+    def column(s, t):
+        return (t * N + source(rank, s)) * SH
+
+    first_t = {}
+
+    def pick(q, s, a, b):
+        have(q, s)
+        listed(q, s)
+        o = offs[s][:, TC * (a - 1):TC * b]
+        k = slice(SH * (a - 1), SH * b)
+        for t in range(a, b + 1):
+            first_t[(s, t)] = a
+        if q is V:
+            V.tensor_copy(T["pk%d" % s][:, k].bitcast(dt.uint32), codes[s][:].bitcast(dt.uint32).indirect(o)
+                          ).then_inc(T.sem["pv%d%d" % (s, a)], 1)
+        else:
+            S.activation(T["pks%d" % s][:, k], scales[s][:].indirect(o), ActivationFunctionType.Copy
+                         ).then_inc(T.sem["ps%d%d" % (s, a)], 1)
+
+    items = [(s, t) for s in range(N - 2) for t in range(R + 1)] + [(s, t) for t in range(R + 1) for s in (N - 2, N - 1)]
+
+    def bank(s, t):
+        b = 512 * (items.index((s, t)) % 8)
+        return T.acc[:, b:b + SH]
+
+    def evac(q, s, t):
+        q.wait_ge(T.sem["mm%d%d" % (s, t)], 1)
+        c = column(s, t)
+        if q is V:
+            V.tensor_copy(T.ys[:, c:c + SH], bank(s, t)).then_inc(T.sem["ev%d%d" % (s, t)], 1)
+        else:
+            S.activation(T.ys[:, c:c + SH], bank(s, t), ActivationFunctionType.Copy).then_inc(T.sem["ev%d%d" % (s, t)], 1)
+
+    for s in range(N - 2):
+        if s > 1:
+            evac(V, s, 0)
+        pick(V, s, 1, 1)
+        if s in (1, 3):
+            evac(V, s - 1, 2)
+        if s < 2:
+            evac(V, s, 0)
+        pick(V, s, 2, 3)
+        if s == 1:
+            evac(V, s, 2)
+    pick(V, 4, 1, 1)
+    evac(V, 3, 2)
+    evac(V, 4, 0)
+    pick(V, 4, 2, 2)
+    pick(V, 5, 1, 1)
+    pick(V, 5, 2, 2)
+    evac(V, 4, 1)
+    pick(V, 4, 3, 3)
+    pick(V, 5, 3, 3)
+    evac(V, 4, 2)
+    evac(V, 4, 3)
+
+    for s in range(N - 2):
+        pick(S, s, 1, 1)
+        if s in (1, 3):
+            evac(S, s - 1, 3)
+        pick(S, s, 2, 3)
+        evac(S, s, 1)
+        if s == 1:
+            evac(S, s, 3)
+    pick(S, 4, 1, 1)
+    evac(S, 3, 3)
+    pick(S, 4, 2, 2)
+    pick(S, 5, 1, 1)
+    evac(S, 5, 0)
+    pick(S, 5, 2, 2)
+    evac(S, 5, 1)
+    pick(S, 4, 3, 3)
+    pick(S, 5, 3, 3)
+    evac(S, 5, 2)
+    evac(S, 5, 3)
+
+    for n, (s, t) in enumerate(items):
+        if n == 0:
+            P.wait_ge(T.sem.xq0, 1)
+        if n == 2:
+            P.wait_ge(T.sem.xq1, 1)
+        if n >= 8:
+            P.wait_ge(T.sem["ev%d%d" % items[n - 8]], 1)
+        if t == 0:
+            have(P, s)
+            rhs, rs = codes[s][:, ND:NP], scales[s][:, ND:NP]
+        else:
+            a = first_t[(s, t)]
+            if a == t:
+                P.wait_ge(T.sem["pv%d%d" % (s, a)], 1)
+                P.wait_ge(T.sem["ps%d%d" % (s, a)], 1)
+            k = slice(SH * (t - 1), SH * t)
+            rhs, rs = T["pk%d" % s][:, k], T["pks%d" % s][:, k]
+        P.matmul_mx(bank(s, t), T.xq[:, 128 * t:128 * t + 128], T.xqs[:, 128 * t:128 * t + 128], rhs, rs, True, True
+                    ).then_inc(T.sem["mm%d%d" % (s, t)], 1)
+
+    Y.wait_ge(T.sem.tab, R)
+    Y.dma_start(T.tabd[:], T.tab[0:32, :]).then_inc(T.sem.tabd, 16)
+    for s in range(2, N):
+        Y.wait_ge(T.sem["ls%d" % s], share)
+        for a in range(4):
+            Y.dma_start(T["off%d" % s][32 * a:32 * a + 32, :], T["lst%d" % s][:]).then_inc(T.sem["rp%d" % s], 16)
+    n = 0
+    for s in range(0, N, 2):
+        for t in range(R + 1):
+            c = min(column(s, t), column(s + 1, t))
+            Y.wait_ge(T.sem["ev%d%d" % (s, t)], 1)
+            Y.wait_ge(T.sem["ev%d%d" % (s + 1, t)], 1)
+            Y.dma_start(T.y[:, c:c + 2 * SH], T.ys[:, c:c + 2 * SH]).then_inc(T.sem.st, 16)
+            n += 16
+    Y.wait_ge(T.sem.st, n)
+
+
+def relay_engines(core, relay, cores, topo):
+    q = cores.index(core)
+    off = topo.engines(core, cores[dest(q, 1)])
+    return [e for e in topo.engines(core, relay) if e not in off]

@@ -7,6 +7,7 @@ NP = ND + SH
 TC = SH // 16
 LC = R * TC
 SLOTS = range(1, N)
+VIA_A, VIA_B = (2, 4), (3, 5)
 
 SCRATCH = {
     "wt": ("sbuf", [128, 4 * NP], "bfloat16"),
@@ -68,10 +69,16 @@ def bits(engines):
 def relays(core, cores, topo):
     q = cores.index(core)
     mine = [c for c in topo.cores_of(core) if c != core]
-    a = [c for c in mine if topo.die(c) != topo.die(core)
-         and all(topo.may_write(c, cores[dest(q, s)]) for s in (3, 5))][0]
-    b = [c for c in mine if topo.die(c) == topo.die(core) and topo.may_write(c, cores[dest(q, 4)])][0]
-    return a, b
+
+    def fit(same, slots):
+        return [c for c in mine if (topo.die(c) == topo.die(core)) == same
+                and all(topo.may_write(c, cores[dest(q, s)]) for s in slots)][0]
+    return fit(False, VIA_A), fit(True, VIA_B)
+
+
+def relay_engines(core, relay, cores, topo):
+    off = topo.engines(core, cores[dest(cores.index(core), 1)])
+    return [e for e in topo.engines(core, relay) if e not in off]
 
 
 def rank_program(g, core, T, topo):
@@ -92,17 +99,18 @@ def rank_program(g, core, T, topo):
             if core not in topo.cores_of(c):
                 continue
             a, b = relays(c, cores, topo)
-            slots = (3, 5) if core == a else (4,) if core == b else ()
+            slots = VIA_A if core == a else VIA_B if core == b else ()
+            full = len(relay_engines(c, core, cores, topo))
             n = 0
             for s in slots:
                 to = cores[dest(q, s)]
                 eng = topo.engines(core, to)
                 if s == slots[0]:
-                    g.wait_ge(T.sem.hc, len(relay_engines(c, core, cores, topo)))
-                n += send(T.hop[:].bitcast(dt.uint8), T["land%d" % s][:].bitcast(dt.uint8), T.sem["ar%d" % s], to, eng)
-                if s == slots[0]:
-                    g.wait_ge(T.sem.hs, len(relay_engines(c, core, cores, topo)))
+                    g.wait_ge(T.sem.hs, full // 2)
                 n += send(T.hops[:], T["lands%d" % s][:], T.sem["ar%d" % s], to, eng)
+                if s == slots[0]:
+                    g.wait_ge(T.sem.hc, full)
+                n += send(T.hop[:].bitcast(dt.uint8), T["land%d" % s][:].bitcast(dt.uint8), T.sem["ar%d" % s], to, eng)
             if n:
                 g.wait_ge(T.sem.sent, n)
         return
@@ -113,48 +121,52 @@ def rank_program(g, core, T, topo):
     off_eng = topo.engines(core, far[1])
 
     Y.dma_start(T.wt[:, 4 * ND:4 * NP], T.wm[:]).then_inc(T.sem.ldw, 16)
-    S.dma_start(T.wt[:, 0:4 * ND], T.dl[:]).then_inc(T.sem.ldw, 16)
     for t in range(R):
         S.dma_start(T.ixa[0:1, CH * t:CH * t + CH], T.ix[:, 2 * t:2 * t + 2]).then_inc(T.sem.ldi, 16)
+    S.dma_start(T.wt[:, 0:4 * ND], T.dl[:]).then_inc(T.sem.ldw, 16)
     h = 256 * (R + 1)
     for i in range(2):
-        Y.dma_start(T.xs[:, h * i:h * i + h], T.x[:, h * i:h * i + h]).then_inc(T.sem["xl%d" % i], 16)
+        S.dma_start(T.xs[:, h * i:h * i + h], T.x[:, h * i:h * i + h]).then_inc(T.sem["xl%d" % i], 16)
 
     g.iota(T.pnum[:], [[0, TC]], 0, 1).then_inc(T.sem.num, 1)
     g.iota(T.mnum[:], [[16, TC]], 0, 0).then_inc(T.sem.num, 1)
     g.wait_ge(T.sem.ldi, 16 * R)
     g.partition_broadcast(T.ixr[:], T.ixa[0:1, :], 128).then_inc(T.sem.pb, 1)
 
-    sent = 0
+    def pools(scale, slots, to):
+        src = T.pools[:] if scale else T.pool[:].bitcast(dt.uint8)
+        tr = []
+        for s in slots:
+            land = T["lands%d" % s][:] if scale else T["land%d" % s][:].bitcast(dt.uint8)
+            tr.append((far[s], topo.engines(core, far[s]), T.sem["ar%d" % s], land))
+        for i, relay in enumerate(to):
+            e = relay_engines(core, relay, cores, topo)
+            w = len(e) // len(to)
+            tr.append((relay, e[w * i:w * i + w], T.sem.hs if scale else T.sem.hc,
+                       T.hops[:] if scale else T.hop[:].bitcast(dt.uint8)))
+        g.remote_dma_fused([RemoteDMATransfer(dst_ids=[at(c)], dma_engine_mask=bits(e), remote_sem=m, srcs=[src], dsts=[d])
+                            for c, e, m, d in tr], local_sem=T.sem.sent)
+        return sum(len(e) for c, e, m, d in tr)
 
-    def two(s, relay):
-        n = 0
-        out, on = topo.engines(core, far[s]), relay_engines(core, relay, cores, topo)
-        for src, land, sem_l, hop, sem_h in (
-                (T.pool[:].bitcast(dt.uint8), T["land%d" % s][:].bitcast(dt.uint8), T.sem["ar%d" % s],
-                 T.hop[:].bitcast(dt.uint8), T.sem.hc),
-                (T.pools[:], T["lands%d" % s][:], T.sem["ar%d" % s], T.hops[:], T.sem.hs)):
-            g.remote_dma_fused([
-                RemoteDMATransfer(dst_ids=[at(far[s])], dma_engine_mask=bits(out), remote_sem=sem_l, srcs=[src], dsts=[land]),
-                RemoteDMATransfer(dst_ids=[at(relay)], dma_engine_mask=bits(on), remote_sem=sem_h, srcs=[src], dsts=[hop]),
-            ], local_sem=T.sem.sent)
-            n += len(out) + len(on)
-        return n
+    share = len(off_eng) // (N - 2)
+
+    def lists():
+        tr = []
+        for i, s in enumerate(range(2, N)):
+            e = topo.engines(core, far[s])[share * i:share * i + share]
+            tr.append(RemoteDMATransfer(dst_ids=[at(far[s])], dma_engine_mask=bits(e), remote_sem=T.sem["ls%d" % s],
+                                        srcs=[T.tabd[:]], dsts=[T["lst%d" % s][:]]))
+        g.remote_dma_fused(tr, local_sem=T.sem.sent)
+        return share * (N - 2)
 
     g.wait_ge(T.sem.qd, 1)
-    sent += two(1, relay_a)
+    sent = pools(True, (1,), (relay_a, relay_b))
+    sent += pools(False, (1,), (relay_a,))
     g.wait_ge(T.sem.tab, R)
     sent += send(T.tab[:], T.off1[:], T.sem.ls1, far[1], off_eng)
-    sent += two(2, relay_b)
+    sent += pools(False, (), (relay_b,))
     g.wait_ge(T.sem.tabd, 16)
-    share = len(off_eng) // (N - 2)
-    tr = []
-    for i, s in enumerate(range(2, N)):
-        e = topo.engines(core, far[s])[share * i:share * i + share]
-        tr.append(RemoteDMATransfer(dst_ids=[at(far[s])], dma_engine_mask=bits(e), remote_sem=T.sem["ls%d" % s],
-                                    srcs=[T.tabd[:]], dsts=[T["lst%d" % s][:]]))
-        sent += len(e)
-    g.remote_dma_fused(tr, local_sem=T.sem.sent)
+    sent += lists()
     g.wait_ge(T.sem.sent, sent)
 
     vc = [0]
@@ -251,48 +263,28 @@ def rank_program(g, core, T, topo):
         else:
             S.activation(T.ys[:, c:c + SH], bank(s, t), ActivationFunctionType.Copy).then_inc(T.sem["ev%d%d" % (s, t)], 1)
 
-    for s in range(N - 2):
-        if s > 1:
-            evac(V, s, 0)
-        pick(V, s, 1, 1)
-        if s in (1, 3):
-            evac(V, s - 1, 2)
-        if s < 2:
-            evac(V, s, 0)
-        pick(V, s, 2, 3)
-        if s == 1:
-            evac(V, s, 2)
-    pick(V, 4, 1, 1)
-    evac(V, 3, 2)
-    evac(V, 4, 0)
-    pick(V, 4, 2, 2)
-    pick(V, 5, 1, 1)
-    pick(V, 5, 2, 2)
-    evac(V, 4, 1)
-    pick(V, 4, 3, 3)
-    pick(V, 5, 3, 3)
-    evac(V, 4, 2)
-    evac(V, 4, 3)
-
-    for s in range(N - 2):
-        pick(S, s, 1, 1)
-        if s in (1, 3):
-            evac(S, s - 1, 3)
-        pick(S, s, 2, 3)
-        evac(S, s, 1)
-        if s == 1:
-            evac(S, s, 3)
-    pick(S, 4, 1, 1)
-    evac(S, 3, 3)
-    pick(S, 4, 2, 2)
-    pick(S, 5, 1, 1)
-    evac(S, 5, 0)
-    pick(S, 5, 2, 2)
-    evac(S, 5, 1)
-    pick(S, 4, 3, 3)
-    pick(S, 5, 3, 3)
-    evac(S, 5, 2)
-    evac(S, 5, 3)
+    for q, a, b in ((V, 0, 2), (S, 1, 3)):
+        for s in range(N - 2):
+            pick(q, s, 1, 1)
+            if s in (1, 3):
+                evac(q, s - 1, b)
+            if q is V:
+                evac(q, s, a)
+            pick(q, s, 2, 3)
+            if q is S:
+                evac(q, s, a)
+            if s == 1:
+                evac(q, s, b)
+        mine = 4 if q is V else 5
+        pick(q, 4, 1, 1)
+        evac(q, 3, b)
+        pick(q, 5, 1, 1)
+        evac(q, mine, 0)
+        for t in (2, 3):
+            pick(q, 4, t, t)
+            pick(q, 5, t, t)
+            evac(q, mine, t - 1)
+        evac(q, mine, 3)
 
     for n, (s, t) in enumerate(items):
         if n == 0:
@@ -329,9 +321,3 @@ def rank_program(g, core, T, topo):
             Y.dma_start(T.y[:, c:c + 2 * SH], T.ys[:, c:c + 2 * SH]).then_inc(T.sem.st, 16)
             n += 16
     Y.wait_ge(T.sem.st, n)
-
-
-def relay_engines(core, relay, cores, topo):
-    q = cores.index(core)
-    off = topo.engines(core, cores[dest(q, 1)])
-    return [e for e in topo.engines(core, relay) if e not in off]

from concourse.bass import DstId, RemoteDMATransfer
from concourse.mybir import dt, AluOpType, ActivationFunctionType

N, SH, CH, R = 6, 192, 32, 3
ND = R * CH
NP = ND + SH
TC = SH // 16
LC = R * TC
SLOTS = range(1, N)
VIA_A, VIA_B = (2, 4), (3, 5)

SCRATCH = {
    "wt": ("sbuf", [128, 4 * NP], "bfloat16"),
    "xs": ("sbuf", [128, 512 * (R + 1)], "bfloat16"),
    "xq": ("sbuf", [128, 128 * (R + 1)], "float8_e4m3fn_x4"),
    "xqs": ("sbuf", [128, 128 * (R + 1)], "uint8"),
    "pool": ("sbuf", [128, NP], "float8_e4m3fn_x4"),
    "pools": ("sbuf", [128, NP], "uint8"),
    "hop": ("sbuf", [128, NP], "float8_e4m3fn_x4"),
    "hops": ("sbuf", [128, NP], "uint8"),
    "ixa": ("sbuf", [128, ND], "int32"),
    "ixr": ("sbuf", [128, ND], "int32"),
    "ixb": ("sbuf", [128, ND], "bfloat16"),
    "stepc": ("sbuf", [128, ND], "bfloat16"),
    "pnum": ("sbuf", [128, TC], "int32"),
    "plow": ("sbuf", [128, TC], "int32"),
    "mnum": ("sbuf", [128, TC], "int32"),
    "ccol": ("sbuf", [128, TC], "float32"),
    "first": ("sbuf", [128, TC], "float32"),
    "ne": ("sbuf", [128, TC * ND], "bfloat16"),
    "stt": ("sbuf", [128, TC * ND], "bfloat16"),
    "tab": ("sbuf", [128, LC], "uint16"),
    "tabd": ("dram", [128, LC // 4], "uint16"),
    "ys": ("sbuf", [128, (R + 1) * N * SH], "float32"),
    "acc": ("psum", [128, 8 * 512], "float32"),
}
for _s in range(N):
    SCRATCH["pk%d" % _s] = ("sbuf", [128, R * SH], "float8_e4m3fn_x4")
    SCRATCH["pks%d" % _s] = ("sbuf", [128, R * SH], "uint8")
for _s in SLOTS:
    SCRATCH["land%d" % _s] = ("sbuf", [128, NP], "float8_e4m3fn_x4")
    SCRATCH["lands%d" % _s] = ("sbuf", [128, NP], "uint8")
    SCRATCH["off%d" % _s] = ("sbuf", [128, LC], "uint16")
    if _s > 1:
        SCRATCH["lst%d" % _s] = ("dram", [128, LC // 4], "uint16")

SEMAPHORES = (["ldw", "ldi", "pb", "num", "vc", "qd", "tab", "tabd", "xl0", "xl1", "xq0", "xq1", "sent", "st", "hc", "hs"]
              + ["ar%d" % s for s in SLOTS] + ["ls%d" % s for s in SLOTS] + ["rp%d" % s for s in SLOTS if s > 1]
              + ["%s%d%d" % (k, s, t) for k in ("pv", "ps") for s in range(N) for t in (1, 2, 3)]
              + ["%s%d%d" % (k, s, t) for k in ("mm", "ev") for s in range(N) for t in range(R + 1)])


def source(r, s):
    a, e = r // 2, r % 2
    return 2 * ((a + s // 2) % (N // 2)) + (e if s % 2 == 0 else 1 - e)


def dest(q, s):
    return [r for r in range(N) if source(r, s) == q][0]


def bits(engines):
    m = 0
    for e in engines:
        m |= 1 << e
    return m


def relays(core, cores, topo):
    q = cores.index(core)
    mine = [c for c in topo.cores_of(core) if c != core]

    def fit(same, slots):
        return [c for c in mine if (topo.die(c) == topo.die(core)) == same
                and all(topo.may_write(c, cores[dest(q, s)]) for s in slots)][0]
    return fit(False, VIA_A), fit(True, VIA_B)


def relay_engines(core, relay, cores, topo):
    off = topo.engines(core, cores[dest(cores.index(core), 1)])
    return [e for e in topo.engines(core, relay) if e not in off]


def rank_program(g, core, T, topo):
    cores = list(T.cores)
    rank = T.rank_of(core)

    def at(c):
        a = topo.addr(c)
        return DstId(rid=a[0], pnc=a[1])

    def send(src, dst, sem, to, engines):
        a = topo.addr(to)
        g.remote_dma(dst, src, sem, T.sem.sent, a[1], a[0], bits(engines))
        return len(engines)

    if rank is None:
        for q, c in enumerate(cores):
            if core not in topo.cores_of(c):
                continue
            a, b = relays(c, cores, topo)
            slots = VIA_A if core == a else VIA_B if core == b else ()
            full = len(relay_engines(c, core, cores, topo))
            n = 0
            for s in slots:
                to = cores[dest(q, s)]
                eng = topo.engines(core, to)
                if s == slots[0]:
                    g.wait_ge(T.sem.hs, full // 2)
                n += send(T.hops[:], T["lands%d" % s][:], T.sem["ar%d" % s], to, eng)
                if s == slots[0]:
                    g.wait_ge(T.sem.hc, full)
                n += send(T.hop[:].bitcast(dt.uint8), T["land%d" % s][:].bitcast(dt.uint8), T.sem["ar%d" % s], to, eng)
            if n:
                g.wait_ge(T.sem.sent, n)
        return

    V, S, P, Y = g.vector, g.scalar, g.tensor, g.sync
    relay_a, relay_b = relays(core, cores, topo)
    far = [None] + [cores[dest(rank, s)] for s in SLOTS]
    off_eng = topo.engines(core, far[1])

    Y.dma_start(T.wt[:, 4 * ND:4 * NP], T.wm[:]).then_inc(T.sem.ldw, 16)
    for t in range(R):
        S.dma_start(T.ixa[0:1, CH * t:CH * t + CH], T.ix[:, 2 * t:2 * t + 2]).then_inc(T.sem.ldi, 16)
    S.dma_start(T.wt[:, 0:4 * ND], T.dl[:]).then_inc(T.sem.ldw, 16)
    h = 256 * (R + 1)
    for i in range(2):
        S.dma_start(T.xs[:, h * i:h * i + h], T.x[:, h * i:h * i + h]).then_inc(T.sem["xl%d" % i], 16)

    g.iota(T.pnum[:], [[0, TC]], 0, 1).then_inc(T.sem.num, 1)
    g.iota(T.mnum[:], [[16, TC]], 0, 0).then_inc(T.sem.num, 1)
    g.wait_ge(T.sem.ldi, 16 * R)
    g.partition_broadcast(T.ixr[:], T.ixa[0:1, :], 128).then_inc(T.sem.pb, 1)

    def pools(scale, slots, to):
        src = T.pools[:] if scale else T.pool[:].bitcast(dt.uint8)
        tr = []
        for s in slots:
            land = T["lands%d" % s][:] if scale else T["land%d" % s][:].bitcast(dt.uint8)
            tr.append((far[s], topo.engines(core, far[s]), T.sem["ar%d" % s], land))
        for i, relay in enumerate(to):
            e = relay_engines(core, relay, cores, topo)
            w = len(e) // len(to)
            tr.append((relay, e[w * i:w * i + w], T.sem.hs if scale else T.sem.hc,
                       T.hops[:] if scale else T.hop[:].bitcast(dt.uint8)))
        g.remote_dma_fused([RemoteDMATransfer(dst_ids=[at(c)], dma_engine_mask=bits(e), remote_sem=m, srcs=[src], dsts=[d])
                            for c, e, m, d in tr], local_sem=T.sem.sent)
        return sum(len(e) for c, e, m, d in tr)

    share = len(off_eng) // (N - 2)

    def lists():
        tr = []
        for i, s in enumerate(range(2, N)):
            e = topo.engines(core, far[s])[share * i:share * i + share]
            tr.append(RemoteDMATransfer(dst_ids=[at(far[s])], dma_engine_mask=bits(e), remote_sem=T.sem["ls%d" % s],
                                        srcs=[T.tabd[:]], dsts=[T["lst%d" % s][:]]))
        g.remote_dma_fused(tr, local_sem=T.sem.sent)
        return share * (N - 2)

    g.wait_ge(T.sem.qd, 1)
    sent = pools(True, (1,), (relay_a, relay_b))
    sent += pools(False, (1,), (relay_a,))
    g.wait_ge(T.sem.tab, R)
    sent += send(T.tab[:], T.off1[:], T.sem.ls1, far[1], off_eng)
    sent += pools(False, (), (relay_b,))
    g.wait_ge(T.sem.tabd, 16)
    sent += lists()
    g.wait_ge(T.sem.sent, sent)

    vc = [0]

    def v(ins):
        vc[0] += 1
        ins.then_inc(T.sem.vc, 1)

    def vwait():
        V.wait_ge(T.sem.vc, vc[0])

    v(V.memset(T.stepc[:, 0:ND:2], 16.0))
    for t in range(R):
        v(V.memset(T.stepc[:, CH * t + 1:CH * t + CH - 1:2], -15.0))
    v(V.memset(T.stepc[:, CH - 1:ND:CH], 1.0))
    V.wait_ge(T.sem.num, 2)
    v(V.tensor_scalar(T.plow[:], T.pnum[:], 15, None, AluOpType.bitwise_and))
    vwait()
    v(V.tensor_tensor(T.ccol[:], T.plow[:], T.mnum[:], AluOpType.add))
    vwait()
    v(V.tensor_scalar(T.first[:], T.ccol[:], -1.0, float(-ND), AluOpType.mult, AluOpType.add))

    V.wait_ge(T.sem.ldw, 32)
    V.quantize_mx(T.pool[:], T.pools[:], T.wt[:]).then_inc(T.sem.qd, 1)

    V.wait_ge(T.sem.pb, 1)
    v(V.tensor_copy(T.ixb[:], T.ixr[:]))
    vwait()
    for m in range(TC):
        v(V.tensor_scalar(T.ne[:, ND * m:ND * m + ND], T.ixb[:], T.ccol[:, m:m + 1], None, AluOpType.not_equal))
    vwait()
    for m in range(TC):
        k = slice(ND * m, ND * m + ND)
        v(V.tensor_tensor_scan(T.stt[:, k], T.ne[:, k], T.stepc[:], T.first[:, m:m + 1], AluOpType.mult, AluOpType.add))
    vwait()
    for t in range(1, R + 1):
        V.tensor_scalar(T.tab[:, TC * (t - 1):TC * t], T.stt[:, CH * t - 1:TC * ND:ND], -1.0, float(CH * t),
                        AluOpType.mult, AluOpType.add).then_inc(T.sem.tab, 1)

    for i in range(2):
        V.wait_ge(T.sem["xl%d" % i], 16)
        k = slice(128 * (R + 1) // 2 * i, 128 * (R + 1) // 2 * (i + 1))
        V.quantize_mx(T.xq[:, k], T.xqs[:, k], T.xs[:, h * i:h * i + h]).then_inc(T.sem["xq%d" % i], 1)

    codes = [T.pool] + [T["land%d" % s] for s in SLOTS]
    scales = [T.pools] + [T["lands%d" % s] for s in SLOTS]
    offs = [T.tab] + [T["off%d" % s] for s in SLOTS]
    eng = len(off_eng)

    def have(q, s):
        if s == 0:
            q.wait_ge(T.sem.qd, 1)
        else:
            q.wait_ge(T.sem["ar%d" % s], 2 * eng)

    def listed(q, s):
        if s == 0:
            q.wait_ge(T.sem.tab, R)
        elif s == 1:
            q.wait_ge(T.sem.ls1, eng)
        else:
            q.wait_ge(T.sem["rp%d" % s], 64)

    def column(s, t):
        return (t * N + source(rank, s)) * SH

    first_t = {}

    def pick(q, s, a, b):
        have(q, s)
        listed(q, s)
        o = offs[s][:, TC * (a - 1):TC * b]
        k = slice(SH * (a - 1), SH * b)
        for t in range(a, b + 1):
            first_t[(s, t)] = a
        if q is V:
            V.tensor_copy(T["pk%d" % s][:, k].bitcast(dt.uint32), codes[s][:].bitcast(dt.uint32).indirect(o)
                          ).then_inc(T.sem["pv%d%d" % (s, a)], 1)
        else:
            S.activation(T["pks%d" % s][:, k], scales[s][:].indirect(o), ActivationFunctionType.Copy
                         ).then_inc(T.sem["ps%d%d" % (s, a)], 1)

    items = [(s, t) for s in range(N - 2) for t in range(R + 1)] + [(s, t) for t in range(R + 1) for s in (N - 2, N - 1)]

    def bank(s, t):
        b = 512 * (items.index((s, t)) % 8)
        return T.acc[:, b:b + SH]

    def evac(q, s, t):
        q.wait_ge(T.sem["mm%d%d" % (s, t)], 1)
        c = column(s, t)
        if q is V:
            V.tensor_copy(T.ys[:, c:c + SH], bank(s, t)).then_inc(T.sem["ev%d%d" % (s, t)], 1)
        else:
            S.activation(T.ys[:, c:c + SH], bank(s, t), ActivationFunctionType.Copy).then_inc(T.sem["ev%d%d" % (s, t)], 1)

    for q, a, b in ((V, 0, 2), (S, 1, 3)):
        for s in range(N - 2):
            pick(q, s, 1, 1)
            if s in (1, 3):
                evac(q, s - 1, b)
            if q is V:
                evac(q, s, a)
            pick(q, s, 2, 3)
            if q is S:
                evac(q, s, a)
            if s == 1:
                evac(q, s, b)
        mine = 4 if q is V else 5
        pick(q, 4, 1, 1)
        evac(q, 3, b)
        pick(q, 5, 1, 1)
        evac(q, mine, 0)
        for t in (2, 3):
            pick(q, 4, t, t)
            pick(q, 5, t, t)
            evac(q, mine, t - 1)
        evac(q, mine, 3)

    for n, (s, t) in enumerate(items):
        if n == 0:
            P.wait_ge(T.sem.xq0, 1)
        if n == 2:
            P.wait_ge(T.sem.xq1, 1)
        if n >= 8:
            P.wait_ge(T.sem["ev%d%d" % items[n - 8]], 1)
        if t == 0:
            have(P, s)
            rhs, rs = codes[s][:, ND:NP], scales[s][:, ND:NP]
        else:
            a = first_t[(s, t)]
            if a == t:
                P.wait_ge(T.sem["pv%d%d" % (s, a)], 1)
                P.wait_ge(T.sem["ps%d%d" % (s, a)], 1)
            k = slice(SH * (t - 1), SH * t)
            rhs, rs = T["pk%d" % s][:, k], T["pks%d" % s][:, k]
        P.matmul_mx(bank(s, t), T.xq[:, 128 * t:128 * t + 128], T.xqs[:, 128 * t:128 * t + 128], rhs, rs, True, True
                    ).then_inc(T.sem["mm%d%d" % (s, t)], 1)

    Y.wait_ge(T.sem.tab, R)
    Y.dma_start(T.tabd[:], T.tab[0:32, :]).then_inc(T.sem.tabd, 16)
    for s in range(2, N):
        Y.wait_ge(T.sem["ls%d" % s], share)
        for a in range(4):
            Y.dma_start(T["off%d" % s][32 * a:32 * a + 32, :], T["lst%d" % s][:]).then_inc(T.sem["rp%d" % s], 16)
    n = 0
    for s in range(0, N, 2):
        for t in range(R + 1):
            c = min(column(s, t), column(s + 1, t))
            Y.wait_ge(T.sem["ev%d%d" % (s, t)], 1)
            Y.wait_ge(T.sem["ev%d%d" % (s + 1, t)], 1)
            Y.dma_start(T.y[:, c:c + 2 * SH], T.ys[:, c:c + 2 * SH]).then_inc(T.sem.st, 16)
            n += 16
    Y.wait_ge(T.sem.st, n)
